import numpy as np
import ml_dtypes


def mxq(x, axis, fmt="e4m3"):
    dtype, down = {"e4m3": (ml_dtypes.float8_e4m3fn, 7), "e5m2": (ml_dtypes.float8_e5m2, 14)}[fmt]
    v = np.moveaxis(np.asarray(x, np.float32).astype(ml_dtypes.bfloat16).astype(np.float64), axis, -1)
    blocks = v.reshape(v.shape[:-1] + (-1, 32))
    amax = np.abs(blocks).max(-1, keepdims=True)
    byte = np.maximum(np.where(amax > 0, np.frexp(amax)[1] - 1 + 127, 0) - down, 1)
    scale = np.exp2(byte - 127.0)
    codes = (blocks / scale).astype(np.float32).astype(dtype).astype(np.float64)
    return np.moveaxis((codes * scale).reshape(v.shape), -1, axis)


WIDE = False


def mx_kscale(k):
    if not WIDE:
        return np.ones(k)
    levels = np.array([10, -10, 5, -5, 0])
    if k % 512:
        return np.exp2(np.random.permutation(np.resize(levels, k // 32))).repeat(32)
    a = np.empty((k // 512, 16))
    for p in range(k // 512):
        a[p, :8] = np.random.permutation(np.resize(levels, 8))
        for g in range(8):
            far = levels[np.abs(levels - a[p, g]) >= 10]
            a[p, g + 8] = far[np.random.randint(len(far))]
    return np.exp2(a.ravel()).repeat(32)


def f64(x):
    return np.asarray(x).astype(np.float64)


def striped(idx):
    return np.tile(idx.reshape(-1, 16).T, (8, 1)).astype(np.uint16)


def unstriped(offs):
    return offs[:16].T.reshape(-1).astype(np.int64)


def striped8(idx):
    return np.concatenate([x.reshape(-1, 16).T for x in idx]).astype(np.uint16)


def runs(offs, k):
    lists = np.stack([offs[16 * r : 16 * r + 16].T.reshape(-1) for r in range(8)]).astype(np.int64)
    return lists[np.arange(k) % 512 // 64]


def pack_weight(w):
    k, n = w.shape
    w = f64(np.asarray(w, np.float32).astype(ml_dtypes.bfloat16)).reshape(k // 32, 32, n)
    amax = np.abs(w).max(1)
    byte = np.clip(np.where(amax > 0, np.frexp(amax)[1] - 1 + 127 - 7, 1), 1, 254)
    scaled = (w * np.exp2(127.0 - byte)[:, None, :]).reshape(k, n).astype(np.float32)
    words = np.ascontiguousarray(scaled.reshape(k // 512, 128, 4, n).transpose(0, 1, 3, 2)).astype(ml_dtypes.float8_e4m3fn).view(np.uint8)
    return words, np.ascontiguousarray(byte.astype(np.uint8).reshape(k // 512, 16, n))


def unpack_weight(words, scales):
    g, p, n, _ = words.shape
    vals = np.ascontiguousarray(words).view(ml_dtypes.float8_e4m3fn).astype(np.float64) * np.repeat(np.exp2(scales.astype(np.float64) - 127.0), 8, axis=1)[..., None]
    return vals.transpose(0, 1, 3, 2).reshape(g * 512, n)

def planes(y):
    n, m = y.shape
    v = y.astype(np.float32).astype(ml_dtypes.bfloat16).astype(np.float64).reshape(n // 32, 32, m)
    top = np.abs(v).max(1)
    byte = np.clip(np.where(top > 0, np.frexp(top)[1] - 1 + 127 - 7, 1), 1, 254)
    codes = (v * np.exp2(127.0 - byte)[:, None, :]).reshape(n, m).astype(np.float32).astype(ml_dtypes.float8_e4m3fn).view(np.uint8)
    words = codes.reshape(n // 512, 128, 4, m).transpose(0, 1, 3, 2)
    return np.ascontiguousarray(words), np.ascontiguousarray(byte.astype(np.uint8).reshape(n // 512, 16, m))


K, T, S, N, H, C = 512, 2048, 512, 512, 512, 512


def setup_inputs():
    n = np.random.standard_normal
    s = mx_kscale(K)[:, None]
    u = mx_kscale(S)
    packed_xT = pack_weight(n((K, T)) * s)
    packed_w1 = pack_weight(n((K, H)) / np.sqrt(K) / s)
    packed_w2 = pack_weight(n((H, N)) / np.sqrt(H) / u[:, None])
    return {
        "x_words": packed_xT[0],
        "x_scales": packed_xT[1],
        "w1_words": packed_w1[0],
        "w1_scales": packed_w1[1],
        "gn": (np.random.uniform(0.5, 1.5, (H, 1)) * u[:, None]).astype(np.float32),
        "w2_words": packed_w2[0],
        "w2_scales": packed_w2[1],
        "gs": (np.random.uniform(0.5, 1.5, (K, 1)) / s).astype(np.float32),
        "offs": striped(np.random.permutation(T)[:S]),
        "n1": striped8(np.stack([np.random.permutation(S) for _ in range(8)])),
        "n2": striped8(np.stack([np.random.permutation(S) for _ in range(8)])),
        "n3": striped8(np.stack([np.random.permutation(S) for _ in range(8)])),
        "n4": striped8(np.stack([np.random.permutation(S) for _ in range(8)])),
        "cand": striped(np.random.permutation(T)[:C]),
        "n5": striped(np.random.permutation(S)),
        "n6": striped(np.random.permutation(S)),
    }


def reference(x_words, x_scales, w1_words, w1_scales, gn, w2_words, w2_scales, gs, offs, n1, n2, n3, n4, cand, n5, n6):
    xq = unpack_weight(x_words, x_scales)[:, unstriped(offs)]
    y = unpack_weight(w1_words, w1_scales).T @ xq
    st = np.maximum(y, y[np.arange(H)[:, None], runs(n1, H)])
    z = f64(gn) * (st[np.arange(H)[:, None], runs(n2, H)] - (0.5 * y))
    a = unpack_weight(w2_words, w2_scales).T @ mxq(z, 0, "e4m3")
    x_cand = unpack_weight(x_words, x_scales)[:, unstriped(cand)]
    st2 = y - (y[np.arange(H)[:, None], runs(n3, H)])
    z2 = f64(gs) * (np.maximum(st2, st2[np.arange(H)[:, None], runs(n4, H)]))
    b = 0.0625 * ((x_cand.T @ mxq(z2, 0, "e4m3")))
    out_0 = np.maximum(a, b[:, unstriped(n6)]) - (np.minimum(a[:, unstriped(n5)], b))
    return (out_0,) + planes(out_0)

from contextlib import ExitStack

import concourse.mybir as mybir

F32 = mybir.dt.float32
BF16 = mybir.dt.bfloat16
I32 = mybir.dt.int32
U32 = mybir.dt.uint32
U16 = mybir.dt.uint16
U8 = mybir.dt.uint8
FP8X4 = mybir.dt.float8_e4m3fn_x4
ALU = mybir.AluOpType
COPY = mybir.ActivationFunctionType.Copy

P = 128
PACK = 4
T = 2048
S = 512
HALF = S // 2
LIST_COLS = S // 16
FUSED = 0
VG5 = 2
I0S = 1
HB = 4
G6ORD = 0
MINP = 1
GDEAL = 0
GSUB = 0
XFIRST = 0
BV = 0
LASTT = 1
ORDER = "A.S.0.1.2 G1.S.0.1.2 c.V.0.1.2 d.V.0.1.2 A.S.1.1.2 G1.S.1.1.2 c.V.1.1.2 d.V.1.1.2 A.S.2.1.2 G1.S.2.1.2 c.V.2.1.2 d.V.2.1.2 A.S.3.1.2 G1.S.3.1.2 c.V.3.1.2 d.V.3.1.2 G3.S.0.1.2 G3.S.1.1.2 G3.S.2.1.2 G3.S.3.1.2 h.V.0.1.2 h.V.1.1.2 h.V.2.1.2 h.V.3.1.2 w2.V.0.1.2 Sz.V.0.1.0 Sz.V.0.1.1 Qz.V.0.1.0 Qz.V.0.1.1 Ma.V.0.2.2 xc.V.0.1.2 xd.V.0.1.2 G4.S.0.1.2 j.V.0.1.2 G4.S.1.1.2 j.V.1.1.2 G4.S.2.1.2 j.V.2.1.2 G4.S.3.1.2 j.V.3.1.2 Sz2.V.0.1.0 Sz2.V.0.1.1 Qz2.V.0.1.0 Qz2.V.0.1.1 a.S.0.1.2 a.S.1.1.2 a.S.2.1.2 a.S.3.1.2 G5.S.0.1.2 G5.S.1.1.2 G5.V.2.1.2 G5.V.3.1.2 Mb.V.0.2.2 b.S.0.1.2 G6.S.0.1.0 b.S.1.1.2 G6.S.1.1.0 Lp.V.2.1.2 Lp.V.3.1.2 L.V.0.2.0 H.V.0.2.0 L.V.0.2.1 b.S.2.1.2 G6.S.2.1.0 b.S.3.1.2 G6.S.3.1.0 R.V.0.2.0 H.V.2.2.0 R.V.2.2.0 I.S.0.1.0 G6.S.0.1.1 G6.S.1.1.1 H.V.0.2.1 Qo.V.0.1.0 R.V.0.2.1 G6.S.2.1.1 G6.S.3.1.1 H.V.2.1.1 H.V.3.1.1 R.V.2.1.1 R.V.3.1.1 I.V.0.1.1 Qo.V.0.1.1"
FLOPS = 3 * 2 * 512 * 512 * 512


def tile_picked_fkcdmaxbhopbhopmx_none_po_kernel(
    tc, x_words, x_scales, w1_words, w1_scales, gn, w2_words, w2_scales, gs,
    offs, n1, n2, n3, n4, cand, n5, n6, out_0, out_1, out_2,
):
    nc = tc.nc
    with ExitStack() as ctx:
        lists = ctx.enter_context(tc.tile_pool(name="lists", bufs=1))
        sb = ctx.enter_context(tc.tile_pool(name="sb", bufs=1))
        ps = ctx.enter_context(tc.psum_pool(name="ps", bufs=1))

        def load_list(name, src):
            tile = lists.tile([P, LIST_COLS], U16, name=name)
            nc.sync.dma_start(tile[:], src)
            return tile

        def load_words(name, src, width):
            tile = sb.tile([P, width], U32, name=name, align_bytes=64)
            nc.sync.dma_start(tile[:].bitcast(I32), src[0].rearrange("p n t -> p (n t)").bitcast(I32))
            return tile

        def scale_tile(name, width, engine):
            tile = sb.tile([P, width], U8, name=name, align_bytes=64)
            engine.memset(tile[:].bitcast(I32), 0)
            return tile

        def load_scales(tile, src, queue=nc.sync):
            for q in range(4):
                queue.dma_start(tile[32 * q : 32 * q + 4, :].bitcast(I32), src[0, 4 * q : 4 * q + 4, :].bitcast(I32))

        def load_gain(name, src):
            tile = sb.tile([P, PACK], F32, name=name)
            nc.sync.dma_start(tile[:], src.rearrange("(p t) o -> p (t o)", t=PACK))
            return tile

        def deal(name, src, dtype, engine=nc.vector):
            tile = sb.tile([P, S], dtype, name=name, align_bytes=64)
            engine.tensor_copy(tile[:].rearrange("p (t m) -> p m t", t=PACK), src[:].rearrange("p (m t) -> p m t", t=PACK))
            return tile

        def pick(name, table, offsets, dtype):
            tile = sb.tile([P, S], dtype, name=name, align_bytes=64)
            nc.vector.tensor_copy(tile[:], table[:].indirect(offsets[:]))
            return tile

        def product(dst, t, cols, lhs_code, lhs_scale, rhs_code, rhs_scale):
            rows = slice(t * P, (t + 1) * P)
            nc.tensor.matmul_mx(
                out=dst, lhsT=lhs_code[:, rows].bitcast(FP8X4), lhsT_scale=lhs_scale[:, rows],
                rhs=rhs_code[:, cols].bitcast(FP8X4), rhs_scale=rhs_scale[:, cols], start=True, stop=True,
            )

        def woven(ap):
            return ap.rearrange("p (c i t) -> p c t i", i=4, t=PACK)

        def planar(ap):
            return ap.rearrange("p t (c i) -> p c t i", i=4)

        halves = [slice(h * HALF, (h + 1) * HALF) for h in range(2)]

        def scale_and_quantize(name, planes, gain, on_scalar):
            rounded = sb.tile([P, S * PACK], BF16, name=name + "_bf", align_bytes=64)
            code = sb.tile([P, S], U32, name=name + "_code", align_bytes=64)
            scale = sb.tile([P, S], U8, name=name + "_scale", align_bytes=64)
            spread = gain[:].unsqueeze(1).unsqueeze(3).to_broadcast([P, HALF // 4, PACK, 4])
            if on_scalar:
                flat = sb.tile([P, PACK, on_scalar * HALF], BF16, name=name + "_flat")
                for t in range(PACK):
                    nc.scalar.activation(flat[:, t, :], planes[:, t, : on_scalar * HALF], COPY, scale=gain[:, t : t + 1])
            for h, cols in enumerate(halves):
                if h < on_scalar:
                    nc.vector.tensor_copy(woven(rounded[:, cols.start * PACK : cols.stop * PACK]), planar(flat[:, :, cols]))
                else:
                    nc.vector.tensor_tensor(
                        woven(rounded[:, cols.start * PACK : cols.stop * PACK]), planar(planes[:, :, cols]), spread, ALU.mult
                    )
            for cols in halves:
                nc.vector.quantize_mx(
                    out=code[:, cols].bitcast(FP8X4), scales=scale[:, cols],
                    in_=rounded[:, cols.start * PACK : cols.stop * PACK],
                )
            return code, scale

        x_scale = scale_tile("x_scale", T, nc.vector)
        w1_scale = scale_tile("w1_scale", S, nc.vector)
        half_y = [sb.tile([P, 2 * S], F32, name="half_y%d" % t) for t in range(PACK)]
        a_sb = sb.tile([P, PACK + 1, S], F32, name="a_sb")
        offs_t = load_list("offs_t", offs)
        load_scales(x_scale, x_scales)
        x_code = sb.tile([P, T], U32, name="x_code", align_bytes=64)
        x_rows = x_words[0].rearrange("p n t -> p (n t)").bitcast(I32)
        nc.sync.dma_start(x_code[:, :512].bitcast(I32), x_rows[:, :512])
        w1_code = load_words("w1_code", w1_words, S)
        nc.sync.dma_start(x_code[:, 512:].bitcast(I32), x_rows[:, 512:])
        load_scales(w1_scale, w1_scales)
        n1_t = load_list("n1_t", n1)
        n2_t = load_list("n2_t", n2)
        cand_t = load_list("cand_t", cand)
        n3_t = load_list("n3_t", n3)
        gn_t = load_gain("gn_t", gn)
        n4_t = load_list("n4_t", n4)
        gs_t = load_gain("gs_t", gs)
        n5_t = load_list("n5_t", n5)
        n6_t = load_list("n6_t", n6)
        for t in range(PACK):
            nc.vector.memset(half_y[t][:, S:], 0.0)
        nc.vector.memset(a_sb[:, PACK, :], 0.0)

        xq_scale = pick("xq_scale", x_scale, offs_t, U8)
        w1d_code = deal("w1d_code", w1_code, U32)
        w1d_scale = deal("w1d_scale", w1_scale, U8)
        xq_code = pick("xq_code", x_code, offs_t, U32)
        y_ps = [ps.tile([P, S], F32, name="yb%d" % t) for t in range(PACK)]
        for t in range(PACK):
            product(y_ps[t][:], t, slice(0, S), w1d_code, w1d_scale, xq_code, xq_scale)

        xc_scale = pick("xc_scale", x_scale, cand_t, U8)
        nc.sync.dma_start(w1_code[:].bitcast(I32), w2_words[0].rearrange("p n t -> p (n t)").bitcast(I32))
        load_scales(w1_scale, w2_scales)


        gs_m2 = sb.tile([P, PACK], F32, name="gs_m2")
        nc.scalar.activation(gs_m2[:], gs_t[:], COPY, scale=-2.0)
        st = [sb.tile([P, 2 * S], F32, name="st%d" % t) for t in range(PACK)]
        st2 = [sb.tile([P, 2 * S], F32, name="u%d" % t) for t in range(PACK)]
        z_pre = sb.tile([P, PACK, S], F32, name="d")
        hop4 = sb.tile([P, PACK, S], F32, name="g4")
        z2_pre = sb.tile([P, PACK, S], F32, name="j")
        hop5 = sb.tile([P, PACK - 2, S], F32, name="g5")
        late5 = {}
        b_sb = sb.tile([P, PACK, S], F32, name="b_sb")
        low = sb.tile([P, PACK, S], F32, name="low")
        hop6 = sb.tile([P, PACK, S], F32, name="g6")
        high = sb.tile([P, PACK, S], F32, name="high")
        result = sb.tile([P, PACK, S], F32, name="res")
        q = {}
        for name in ("z", "z2", "o"):
            q[name] = (
                sb.tile([P, S * PACK], BF16, align_bytes=64, name=name + "bf"),
                sb.tile([P, S], U32, align_bytes=64, name=name + "code"),
                sb.tile([P, S], U8, align_bytes=64, name=name + "scale"),
            )
        a_ps = [ps.tile([P, S], F32, name="ab%d" % t) for t in range(PACK)]
        b_ps = {}
        w = {}
        out_rows = out_0.rearrange("(p t) c -> p t c", t=PACK)
        out_words = out_1[0].rearrange("p n t -> p (n t)").bitcast(I32)
        eng = {"V": nc.vector, "G": nc.gpsimd}

        def gather(e, dst, src):
            if e == "S":
                nc.scalar.activation(dst, src, COPY)
            else:
                nc.vector.tensor_copy(dst, src)

        def evac(e, dst, src, f):
            if e == "S":
                nc.scalar.activation(dst, src, COPY, scale=f)
            else:
                nc.vector.tensor_scalar(dst, src, f, None, ALU.mult)

        def g5(rows, cols):
            if rows.start >= PACK - 2:
                return late5[0][:, rows.start - (PACK - 2) : rows.stop - (PACK - 2), cols]
            return hop5[:, rows, cols]

        def wide(cols):
            return slice(cols.start * PACK, cols.stop * PACK)

        def step(op, e, t, n, h):
            rows = slice(t, t + n)
            cols = halves[h] if h < 2 else slice(0, S)
            lc = slice(cols.start // 16, cols.stop // 16)
            if op == "w2":
                w["w2c"] = deal("w2d_code", w1_code, U32, eng[e])
                w["w2s"] = deal("w2d_scale", w1_scale, U8, eng[e])
            elif op == "xc":
                w["xc"] = pick("xc_code", x_code, cand_t, U32)
            elif op == "xd":
                w["xcc"] = deal("xcd_code", w["xc"], U32)
                w["xcs"] = deal("xcd_scale", xc_scale, U8)
            elif op == "A":
                evac(e, half_y[t][:, :S], y_ps[t][:], 0.5)
            elif op == "G1":
                gather(e, st[t][:, S:], half_y[t][:].indirect(n1_t[:]))
            elif op == "c":
                nc.vector.scalar_tensor_tensor(st[t][:, :S], st[t][:, S:], 2.0, y_ps[t][:], ALU.mult, ALU.max)
            elif op == "d":
                nc.vector.tensor_tensor(z_pre[:, t, :], st[t][:].indirect(n2_t[:]), half_y[t][:, :S], ALU.subtract)
            elif op == "G3":
                gather(e, st2[t][:, S:], half_y[t][:].indirect(n3_t[:]))
            elif op == "B":
                nc.sync.dma_start(st2[t][:, S:], half_y[t][:, :S])
            elif op == "hf":
                nc.vector.tensor_tensor(st2[t][:, :S], half_y[t][:].indirect(n3_t[:]), st2[t][:, S:], ALU.subtract)
            elif op == "h":
                eng[e].tensor_tensor(st2[t][:, :S], st2[t][:, S:], half_y[t][:, :S], ALU.subtract)
            elif op == "G4":
                gather(e, hop4[:, t, :], st2[t][:].indirect(n4_t[:]))
            elif op == "j":
                nc.vector.tensor_tensor(z2_pre[:, t, :], hop4[:, t, :], st2[t][:, :S], ALU.min)
            elif op in ("Sz", "Sz2"):
                src, gain = (z_pre, gn_t) if op == "Sz" else (z2_pre, gs_m2)
                spread = gain[:].unsqueeze(1).unsqueeze(3).to_broadcast([P, (cols.stop - cols.start) // 4, PACK, 4])
                nc.vector.tensor_tensor(woven(q[op[1:]][0][:, wide(cols)]), planar(src[:, :, cols]), spread, ALU.mult)
            elif op in ("Qz", "Qz2", "Qo"):
                r, c, s8 = q[op[1:]]
                nc.vector.quantize_mx(out=c[:, cols].bitcast(FP8X4), scales=s8[:, cols], in_=r[:, wide(cols)])
                if op == "Qo":
                    nc.sync.dma_start(out_words[:, cols], c[:, cols].bitcast(I32))
            elif op == "Ma":
                for u in range(PACK):
                    for cc in halves if n == 2 else [cols]:
                        product(a_ps[u][:, cc], u, cc, w["w2c"], w["w2s"], q["z"][1], q["z"][2])
            elif op == "Mb":
                for u in range(PACK):
                    if u not in b_ps:
                        b_ps[u] = ps.tile([P, S], F32, name="yb%d" % u)
                    for cc in halves if n == 2 else [cols]:
                        product(b_ps[u][:, cc], u, cc, w["xcc"], w["xcs"], q["z2"][1], q["z2"][2])
            elif op == "a":
                evac(e, a_sb[:, t, :], a_ps[t][:], 1.0)
            elif op == "G5":
                if t >= PACK - 2 and not late5:
                    late5[0] = sb.tile([P, 2, S], F32, name="g5l", tag="z2bf", align_bytes=64)
                gather(e, g5(slice(t, t + 1), slice(0, S))[:, 0, :], a_sb[:, t : t + 2, :].rearrange("p t c -> p (t c)").indirect(n5_t[:]))
            elif op == "b":
                evac(e, b_sb[:, t, :], b_ps[t][:], 0.0625)
            elif op == "Lp":
                nc.vector.scalar_tensor_tensor(low[:, t, cols], b_ps[t][:, cols], 0.0625, g5(rows, cols)[:, 0, :], ALU.mult, ALU.min)
            elif op == "L":
                nc.vector.tensor_tensor(low[:, rows, cols], b_sb[:, rows, cols], g5(rows, cols), ALU.min)
            elif op == "G6":
                gather(e, hop6[:, t, cols], b_sb[:, t, :].indirect(n6_t[:, lc]))
            elif op == "H":
                nc.vector.tensor_tensor(high[:, rows, cols], hop6[:, rows, cols], a_sb[:, rows, cols], ALU.max)
            elif op == "R":
                eng[e].tensor_tensor(result[:, rows, cols], high[:, rows, cols], low[:, rows, cols], ALU.subtract)
                nc.sync.dma_start(out_rows[:, rows, cols], result[:, rows, cols])
            elif op == "I":
                if e == "S":
                    nc.scalar.copy(woven(q["o"][0][:, wide(cols)]), planar(result[:, :, cols]))
                else:
                    nc.vector.tensor_copy(woven(q["o"][0][:, wide(cols)]), planar(result[:, :, cols]))

        for item in ORDER.split():
            f = item.split(".")
            step(f[0], f[1], int(f[2]), int(f[3]), int(f[4]))
        for g in range(4):
            nc.sync.dma_start(out_2[0, 4 * g : 4 * g + 4, :].bitcast(I32), q["o"][2][32 * g : 32 * g + 4, :].bitcast(I32))
